import numpy as np, ml_dtypes
CORES = [50,106,114,52,108,116]
N = 6
R, C = 8, 128
def setup_inputs(rng):
    return {"x": rng.standard_normal((N, 128, C), dtype=np.float32).astype(ml_dtypes.bfloat16), "u": rng.standard_normal((N, R, 128), dtype=np.float32).astype(ml_dtypes.bfloat16), "v": rng.standard_normal((N, R, C), dtype=np.float32).astype(ml_dtypes.bfloat16)}
def setup_inputs_big(rng):
    d = setup_inputs(rng)
    for k in ("u", "v"): d[k] = (d[k].astype(np.float32) * 1024.0).astype(d[k].dtype)
    for k in ("x",): d[k] = (d[k].astype(np.float32) * 1024.0 ** 2).astype(d[k].dtype)
    return d
def setup_inputs_small(rng):
    d = setup_inputs(rng)
    for k in ("u", "v"): d[k] = (d[k].astype(np.float32) * (1 / 1024.0)).astype(d[k].dtype)
    for k in ("x",): d[k] = (d[k].astype(np.float32) * (1 / 1024.0 ** 2)).astype(d[k].dtype)
    return d
def setup_inputs_apart(rng):
    d = setup_inputs(rng)
    f = (10.0 ** rng.permutation(np.linspace(-1.5, 1.5, N))).astype(np.float32).reshape(N, 1, 1)
    for k in ("u", "v"): d[k] = (d[k].astype(np.float32) * f).astype(d[k].dtype)
    for k in ("x",): d[k] = (d[k].astype(np.float32) * f * f).astype(d[k].dtype)
    return d
def reference(x, u, v):
    X, U, V = x.astype(np.float64), u.astype(np.float64), v.astype(np.float64)
    s = V.sum(axis=0)
    return {"y": np.stack([X[r] + U[r].T @ s for r in range(N)]).astype(ml_dtypes.bfloat16 if x.dtype != np.float64 else np.float64)}

from concourse.bass import DstId, RemoteDMATransfer
from concourse.mybir import AluOpType

R, C = 8, 128
PER_CHIP = 2
OTHER_CHIPS = 2

SCRATCH = {
    "pair": ("dram", [PER_CHIP, 128, R * C // 128], "bfloat16"),
    "land": ("dram", [OTHER_CHIPS, 128, R * C // 128], "bfloat16"),
    "urep": ("sbuf", [128, 128], "bfloat16"),
    "rhs": ("sbuf", [128, 2 * C], "bfloat16"),
    "xsb": ("sbuf", [128, C], "bfloat16"),
    "ysb": ("sbuf", [128, C], "bfloat16"),
    "acc": ("psum", [128, C], "float32"),
}
SEMAPHORES = ["ldv", "ldu", "ldx", "part", "late", "sent1", "sent2", "rel1", "rel2", "mm", "vs", "st"]


def _bits(m):
    return [1 << i for i in range(m.bit_length()) if (m >> i) & 1]


def rank_program(g, core, T, topo):
    if T.rank_of(core) is None:
        return
    S = T.sem
    chips = sorted({topo.chip(c) for c in T.cores})
    mine = topo.chip(core)
    partner = [c for c in T.cores if topo.chip(c) == mine and c != core][0]
    away = [c for c in T.cores if topo.chip(c) != mine]

    def reaches_all(c):
        return all(topo.may_write(c, d) for d in T.cores if topo.chip(d) != topo.chip(c))

    def porter_of(ch):
        return [c for c in T.cores if topo.chip(c) == ch and reaches_all(c)][0]

    def lanes_of(p):
        far = [d for d in T.cores if topo.chip(d) != topo.chip(p)]
        m = topo.mask(p, [c for c in T.cores if topo.chip(c) == topo.chip(p) and c != p][0])
        for d in far:
            m &= topo.mask(p, d)
        b = _bits(m)
        return b[::len(b) // len(far)][:len(far)]

    porter = porter_of(mine)
    am_porter = core == porter
    lanes = lanes_of(porter)
    to_partner = sum(lanes) if am_porter else _bits(topo.mask(core, partner))[0]
    from_partner = 1 if am_porter else len(lanes)

    g.sync.dma_start(T.pair[0], T.v[:]).then_inc(S.ldv, 16)
    g.sync.dma_start(T.urep[0:R, :], T.u[:]).then_inc(S.ldu, 16)
    g.sync.dma_start(T.urep[R:2 * R, :], T.u[:]).then_inc(S.ldu, 16)
    g.sync.dma_start(T.xsb[:], T.x[:]).then_inc(S.ldx, 16)

    g.wait_ge(S.ldv, 16)
    rid, pid, _ = topo.addr(partner)
    g.remote_dma(out_ap=T.pair[1], in_ap=T.pair[0], remote_sem=S.part, local_sem=S.sent1,
                 pid=pid, routing_id=rid, dma_engine_mask=to_partner)
    if am_porter:
        g.wait_ge(S.part, from_partner)
        transfers = []
        for lane, d in zip(lanes, away):
            rid, pid, _ = topo.addr(d)
            slot = [ch for ch in chips if ch != topo.chip(d)].index(mine)
            transfers.append(RemoteDMATransfer(
                dst_ids=[DstId(rid=rid, pnc=pid)], dma_engine_mask=lane, remote_sem=S.late,
                srcs=[T.pair[0], T.pair[1]], dsts=[T.land[slot]], alu_op=1))
        g.remote_dma_fused(transfers, local_sem=S.sent2)

    g.scalar.wait_ge(S.ldv, 16)
    g.scalar.wait_ge(S.part, from_partner)
    g.scalar.dma_start(T.rhs[0:PER_CHIP * R, 0:C], T.pair[:]).then_inc(S.rel1, 16)
    g.scalar.wait_ge(S.late, OTHER_CHIPS)
    g.scalar.dma_start(T.rhs[0:OTHER_CHIPS * R, C:2 * C], T.land[:]).then_inc(S.rel2, 16)

    g.tensor.wait_ge(S.ldu, 32)
    g.tensor.wait_ge(S.rel1, 16)
    g.tensor.matmul(out=T.acc[:], lhsT=T.urep[0:PER_CHIP * R, :], rhs=T.rhs[0:PER_CHIP * R, 0:C],
                    start=True, stop=False)
    g.tensor.wait_ge(S.rel2, 16)
    g.tensor.matmul(out=T.acc[:], lhsT=T.urep[0:OTHER_CHIPS * R, :], rhs=T.rhs[0:OTHER_CHIPS * R, C:2 * C],
                    start=False, stop=True).then_inc(S.mm, 1)

    g.vector.wait_ge(S.ldx, 16)
    g.vector.wait_ge(S.mm, 1)
    g.vector.tensor_tensor(out=T.ysb[:], in0=T.acc[:], in1=T.xsb[:], op=AluOpType.add).then_inc(S.vs, 1)
    g.sync.wait_ge(S.vs, 1)
    g.sync.dma_start(T.y[:], T.ysb[:]).then_inc(S.st, 16)
    g.sync.wait_ge(S.st, 16)

    g.wait_ge(S.sent1, len(_bits(to_partner)))
    if am_porter:
        g.wait_ge(S.sent2, len(lanes))
